import numpy as np, ml_dtypes
CORES = [4,20,36,52,68,84,100,116,132,148,164,180,196,212,228,244]
N = 16
C = 64
def setup_inputs(rng):
    return {"x": rng.standard_normal((N, 128, C), dtype=np.float32).astype(ml_dtypes.bfloat16)}
def setup_inputs_big(rng):
    d = setup_inputs(rng)
    for k in ("x",): d[k] = (d[k].astype(np.float32) * 1048576.0).astype(d[k].dtype)
    return d
def setup_inputs_small(rng):
    d = setup_inputs(rng)
    for k in ("x",): d[k] = (d[k].astype(np.float32) * (1 / 1048576.0)).astype(d[k].dtype)
    return d
def setup_inputs_apart(rng):
    d = setup_inputs(rng)
    f = (10.0 ** rng.permutation(np.linspace(-1.5, 1.5, N))).astype(np.float32).reshape(N, 1, 1)
    for k in ("x",): d[k] = (d[k].astype(np.float32) * f).astype(d[k].dtype)
    return d
def reference(x):
    X = x.astype(np.float64)
    y = np.stack([sum(np.maximum(X[r] - X[s], 0.0) for s in range(N)) for r in range(N)])
    return {"y": y.astype(ml_dtypes.bfloat16)}

@@ -1,0 +1,97 @@
+from concourse.bass import DstId, RemoteDMATransfer
+from concourse.mybir import AluOpType
+
+N = 16
+CH = 8
+WB = 72
+NBLK = 4
+
+SCRATCH = {
+    "gath": ("dram", [N, 128, 64], "bfloat16"),
+    "G": ("sbuf", [128, 1024], "bfloat16"),
+    "D": ("sbuf", [128, 1024], "bfloat16"),
+    "X8": ("sbuf", [128, 1024], "bfloat16"),
+    "ZZ": ("sbuf", [128, 1024], "bfloat16"),
+    "BN": ("sbuf", [128, WB], "bfloat16"),
+    "B16": ("sbuf", [128, WB], "bfloat16"),
+    "R": ("sbuf", [128, 128], "bfloat16"),
+    "YS": ("sbuf", [128, 128], "bfloat16"),
+    "XP0": ("psum", [128, 512], "float32"),
+    "XP1": ("psum", [128, 512], "float32"),
+    "ACC": ("psum", [128, 512], "float32"),
+}
+SEMAPHORES = ["own", "sent", "arr", "zero", "fill", "cst", "xp", "gl", "v0", "v1", "v2", "v3", "mm", "yc", "st"]
+
+
+def rank_program(g, core, T, topo):
+    rank = T.rank_of(core)
+    if rank is None:
+        return
+    S = T.sem
+    cores = T.cores
+
+    g.sync.dma_start(T.gath[0], T.x[:]).then_inc(S.own, 16)
+    g.sync.dma_start(T.X8[0:CH, :], T.x[:]).then_inc(S.cst, 16)
+
+    g.vector.memset(T.ZZ[:, :], 0.0).then_inc(S.zero, 1)
+    g.vector.wait_ge(S.zero, 1)
+    g.vector.memset(T.ZZ[0:16, 7:CH * WB:WB + 8], -1.0).then_inc(S.fill, 1)
+    g.vector.memset(T.ZZ[32:33, 7:CH * WB:WB + 8], 16.0).then_inc(S.fill, 1)
+    for k in range(CH):
+        g.vector.memset(T.ZZ[64:65, 129 * k:128 * (k + 1):CH], 1.0).then_inc(S.fill, 1)
+
+    g.scalar.wait_ge(S.fill, 2 + CH)
+    g.scalar.dma_start(T.R[0:CH, :], T.ZZ[64:65, 0:CH * 128]).then_inc(S.cst, 16)
+    g.scalar.dma_start(T.B16[0:CH, :], T.ZZ[32:33, 0:CH * WB]).then_inc(S.cst, 16)
+    g.scalar.dma_start(T.BN[:, :], T.ZZ[0:16, 0:CH * WB]).then_inc(S.cst, 16)
+
+    dests = [cores[(rank + k) % N] for k in range(N)]
+    common = topo.mask(core, dests[1])
+    for k in range(2, N):
+        common &= topo.mask(core, dests[k])
+    engines = [e for e in range(16) if (common >> e) & 1]
+    transfers = []
+    for i, e in enumerate(engines):
+        ks = list(range(1 + i, N, len(engines)))
+        if not ks:
+            continue
+        ids = []
+        for k in ks:
+            rid, pid = topo.addr(dests[k], core)
+            ids.append(DstId(rid=rid, pnc=pid))
+        transfers.append(RemoteDMATransfer(dst_ids=ids, dma_engine_mask=1 << e, remote_sem=S.arr,
+                                           srcs=[T.gath[0]], dsts=[T.gath[k] for k in ks], alu_op=0))
+    g.wait_ge(S.own, 16)
+    g.remote_dma_fused(transfers, local_sem=S.sent)
+
+    g.tensor.wait_ge(S.cst, 64)
+    g.tensor.matmul(T.XP0[:, :], T.R[0:CH, :], T.X8[0:CH, 0:512], True, True).then_inc(S.xp, 1)
+    g.tensor.matmul(T.XP1[:, :], T.R[0:CH, :], T.X8[0:CH, 512:1024], True, True).then_inc(S.xp, 1)
+    acc = T.ACC[0:64, 0:128]
+    for b in range(8):
+        g.tensor.matmul(acc, T.B16[0:CH, 7 - b:71 - b], T.X8[0:CH, 128 * b:128 * b + 128], b == 0, False)
+
+    g.sync.wait_ge(S.own, 16)
+    g.sync.wait_ge(S.arr, N - 1)
+    g.sync.dma_start(T.G[:, :], T.gath[:]).then_inc(S.gl, 16)
+
+    g.vector.wait_ge(S.xp, 2)
+    g.vector.wait_ge(S.gl, 16)
+    wblk = 1024 // NBLK
+    for i in range(NBLK):
+        a = i * wblk
+        xp = T.XP0 if a < 512 else T.XP1
+        g.vector.tensor_tensor(T.D[:, a:a + wblk], T.G[:, a:a + wblk], xp[:, a % 512:a % 512 + wblk],
+                               AluOpType.min).then_inc(S["v%d" % i], 1)
+    for i in range(NBLK):
+        g.tensor.wait_ge(S["v%d" % i], 1)
+        for b in range(i * wblk // 128, (i + 1) * wblk // 128):
+            mm = g.tensor.matmul(acc, T.BN[:, 7 - b:71 - b], T.D[:, 128 * b:128 * b + 128], False, b == 7)
+    mm.then_inc(S.mm, 1)
+
+    g.vector.wait_ge(S.mm, 1)
+    g.vector.tensor_copy(T.YS[0:64, :], acc).then_inc(S.yc, 1)
+    g.sync.wait_ge(S.yc, 1)
+    g.sync.dma_start(T.y[:], T.YS[0:64, :]).then_inc(S.st, 16)
+    g.sync.wait_ge(S.st, 16)
+    g.wait_ge(S.sent, len(transfers))

@@ -2,25 +2,29 @@ from concourse.bass import DstId, RemoteDMATransfer
 from concourse.mybir import AluOpType
 
 N = 16
-CH = 8
-WB = 72
-NBLK = 4
+CH = 16
+L = 512
+WB = 68
+ZW = CH * WB
+BLOCKS_B = [(0, 256), (256, 384), (384, 512)]
 
 SCRATCH = {
     "gath": ("dram", [N, 128, 64], "bfloat16"),
-    "G": ("sbuf", [128, 1024], "bfloat16"),
-    "D": ("sbuf", [128, 1024], "bfloat16"),
-    "X8": ("sbuf", [128, 1024], "bfloat16"),
-    "ZZ": ("sbuf", [128, 1024], "bfloat16"),
+    "GA": ("sbuf", [128, L], "bfloat16"),
+    "GB": ("sbuf", [128, L], "bfloat16"),
+    "DA": ("sbuf", [128, L], "bfloat16"),
+    "DB": ("sbuf", [128, L], "bfloat16"),
+    "X16": ("sbuf", [128, L], "bfloat16"),
+    "ZZ": ("sbuf", [128, ZW], "bfloat16"),
     "BN": ("sbuf", [128, WB], "bfloat16"),
-    "B16": ("sbuf", [128, WB], "bfloat16"),
+    "B15": ("sbuf", [128, WB], "bfloat16"),
     "R": ("sbuf", [128, 128], "bfloat16"),
     "YS": ("sbuf", [128, 128], "bfloat16"),
-    "XP0": ("psum", [128, 512], "float32"),
-    "XP1": ("psum", [128, 512], "float32"),
+    "XP": ("psum", [128, L], "float32"),
     "ACC": ("psum", [128, 512], "float32"),
 }
-SEMAPHORES = ["own", "sent", "arr", "zero", "fill", "cst", "xp", "gl", "v0", "v1", "v2", "v3", "mm", "yc", "st"]
+SEMAPHORES = ["own", "sent", "arrA", "arrB", "zero", "fill", "cst", "xp", "glA", "glB", "vA", "v0", "v1", "v2",
+              "mm", "yc", "st"]
 
 
 def rank_program(g, core, T, topo):
@@ -31,62 +35,68 @@ def rank_program(g, core, T, topo):
     cores = T.cores
 
     g.sync.dma_start(T.gath[0], T.x[:]).then_inc(S.own, 16)
-    g.sync.dma_start(T.X8[0:CH, :], T.x[:]).then_inc(S.cst, 16)
+    g.sync.dma_start(T.X16[0:CH, :], T.x[:]).then_inc(S.cst, 16)
 
     g.vector.memset(T.ZZ[:, :], 0.0).then_inc(S.zero, 1)
     g.vector.wait_ge(S.zero, 1)
-    g.vector.memset(T.ZZ[0:16, 7:CH * WB:WB + 8], -1.0).then_inc(S.fill, 1)
-    g.vector.memset(T.ZZ[32:33, 7:CH * WB:WB + 8], 16.0).then_inc(S.fill, 1)
-    for k in range(CH):
-        g.vector.memset(T.ZZ[64:65, 129 * k:128 * (k + 1):CH], 1.0).then_inc(S.fill, 1)
+    for s in range(8):
+        a = 8 + 16 * s
+        g.vector.memset(T.ZZ[64:65, a:a + 129 * 7 + 1:129], 1.0).then_inc(S.fill, 1)
+    g.vector.memset(T.ZZ[32:33, 3:ZW:WB + 4], 15.0).then_inc(S.fill, 1)
+    g.vector.memset(T.ZZ[0:8, 3:ZW:WB + 4], -1.0).then_inc(S.fill, 1)
 
-    g.scalar.wait_ge(S.fill, 2 + CH)
-    g.scalar.dma_start(T.R[0:CH, :], T.ZZ[64:65, 0:CH * 128]).then_inc(S.cst, 16)
-    g.scalar.dma_start(T.B16[0:CH, :], T.ZZ[32:33, 0:CH * WB]).then_inc(S.cst, 16)
-    g.scalar.dma_start(T.BN[:, :], T.ZZ[0:16, 0:CH * WB]).then_inc(S.cst, 16)
+    g.scalar.wait_ge(S.fill, 10)
+    g.scalar.dma_start(T.R[0:8, :], T.ZZ[64:65, 8:1032]).then_inc(S.cst, 16)
+    g.scalar.dma_start(T.R[8:16, :], T.ZZ[64:65, 0:1024]).then_inc(S.cst, 16)
+    g.scalar.dma_start(T.B15[0:CH, :], T.ZZ[32:33, :]).then_inc(S.cst, 16)
+    g.scalar.dma_start(T.BN[:, :], T.ZZ[0:8, :]).then_inc(S.cst, 16)
 
     dests = [cores[(rank + k) % N] for k in range(N)]
     common = topo.mask(core, dests[1])
     for k in range(2, N):
         common &= topo.mask(core, dests[k])
     engines = [e for e in range(16) if (common >> e) & 1]
-    transfers = []
-    for i, e in enumerate(engines):
-        ks = list(range(1 + i, N, len(engines)))
-        if not ks:
-            continue
-        ids = []
-        for k in ks:
+    nA = len(engines)
+    nB = N - 1 - nA
+
+    def wave(ks, sem):
+        trs = []
+        for e, k in zip(engines, ks):
             rid, pid = topo.addr(dests[k], core)
-            ids.append(DstId(rid=rid, pnc=pid))
-        transfers.append(RemoteDMATransfer(dst_ids=ids, dma_engine_mask=1 << e, remote_sem=S.arr,
-                                           srcs=[T.gath[0]], dsts=[T.gath[k] for k in ks], alu_op=0))
+            trs.append(RemoteDMATransfer(dst_ids=[DstId(rid=rid, pnc=pid)], dma_engine_mask=1 << e, remote_sem=sem,
+                                         srcs=[T.gath[0]], dsts=[T.gath[k]], alu_op=0))
+        g.remote_dma_fused(trs, local_sem=S.sent)
+
     g.wait_ge(S.own, 16)
-    g.remote_dma_fused(transfers, local_sem=S.sent)
+    wave(range(1, 1 + nA), S.arrA)
+    wave(range(1 + nA, N), S.arrB)
 
-    g.tensor.wait_ge(S.cst, 64)
-    g.tensor.matmul(T.XP0[:, :], T.R[0:CH, :], T.X8[0:CH, 0:512], True, True).then_inc(S.xp, 1)
-    g.tensor.matmul(T.XP1[:, :], T.R[0:CH, :], T.X8[0:CH, 512:1024], True, True).then_inc(S.xp, 1)
+    g.tensor.wait_ge(S.cst, 80)
+    g.tensor.matmul(T.XP[:, :], T.R[0:CH, :], T.X16[0:CH, :], True, True).then_inc(S.xp, 1)
     acc = T.ACC[0:64, 0:128]
-    for b in range(8):
-        g.tensor.matmul(acc, T.B16[0:CH, 7 - b:71 - b], T.X8[0:CH, 128 * b:128 * b + 128], b == 0, False)
+    for b in range(4):
+        g.tensor.matmul(acc, T.B15[0:CH, 3 - b:67 - b], T.X16[0:CH, 128 * b:128 * b + 128], b == 0, False)
 
-    g.sync.wait_ge(S.own, 16)
-    g.sync.wait_ge(S.arr, N - 1)
-    g.sync.dma_start(T.G[:, :], T.gath[:]).then_inc(S.gl, 16)
+    pA, pB = CH * nA, CH * nB
+    g.sync.wait_ge(S.arrA, nA)
+    g.sync.dma_start(T.GA[0:pA, :], T.gath[1:1 + nA]).then_inc(S.glA, 16)
+    g.scalar.wait_ge(S.arrB, nB)
+    g.scalar.dma_start(T.GB[0:pB, :], T.gath[1 + nA:N]).then_inc(S.glB, 16)
 
-    g.vector.wait_ge(S.xp, 2)
-    g.vector.wait_ge(S.gl, 16)
-    wblk = 1024 // NBLK
-    for i in range(NBLK):
-        a = i * wblk
-        xp = T.XP0 if a < 512 else T.XP1
-        g.vector.tensor_tensor(T.D[:, a:a + wblk], T.G[:, a:a + wblk], xp[:, a % 512:a % 512 + wblk],
-                               AluOpType.min).then_inc(S["v%d" % i], 1)
-    for i in range(NBLK):
+    g.vector.wait_ge(S.xp, 1)
+    g.vector.wait_ge(S.glA, 16)
+    g.vector.tensor_tensor(T.DA[0:pA, :], T.GA[0:pA, :], T.XP[0:pA, :], AluOpType.min).then_inc(S.vA, 1)
+    g.vector.wait_ge(S.glB, 16)
+    for i, (a, z) in enumerate(BLOCKS_B):
+        g.vector.tensor_tensor(T.DB[0:pB, a:z], T.GB[0:pB, a:z], T.XP[0:pB, a:z], AluOpType.min).then_inc(S["v%d" % i], 1)
+
+    g.tensor.wait_ge(S.vA, 1)
+    for b in range(4):
+        g.tensor.matmul(acc, T.BN[0:pA, 3 - b:67 - b], T.DA[0:pA, 128 * b:128 * b + 128], False, False)
+    for i, (a, z) in enumerate(BLOCKS_B):
         g.tensor.wait_ge(S["v%d" % i], 1)
-        for b in range(i * wblk // 128, (i + 1) * wblk // 128):
-            mm = g.tensor.matmul(acc, T.BN[:, 7 - b:71 - b], T.D[:, 128 * b:128 * b + 128], False, b == 7)
+        for b in range(a // 128, z // 128):
+            mm = g.tensor.matmul(acc, T.BN[0:pB, 3 - b:67 - b], T.DB[0:pB, 128 * b:128 * b + 128], False, b == 3)
     mm.then_inc(S.mm, 1)
 
     g.vector.wait_ge(S.mm, 1)
@@ -94,4 +104,4 @@ def rank_program(g, core, T, topo):
     g.sync.wait_ge(S.yc, 1)
     g.sync.dma_start(T.y[:], T.YS[0:64, :]).then_inc(S.st, 16)
     g.sync.wait_ge(S.st, 16)
-    g.wait_ge(S.sent, len(transfers))
+    g.wait_ge(S.sent, N - 1)

@@ -6,24 +6,40 @@ CH = 16
 L = 512
 WB = 68
 ZW = CH * WB
-BLOCKS_B = [(0, 256), (256, 384), (384, 512)]
 
 SCRATCH = {
     "gath": ("dram", [N, 128, 64], "bfloat16"),
-    "GA": ("sbuf", [128, L], "bfloat16"),
-    "GB": ("sbuf", [128, L], "bfloat16"),
-    "DA": ("sbuf", [128, L], "bfloat16"),
-    "DB": ("sbuf", [128, L], "bfloat16"),
-    "X16": ("sbuf", [128, L], "bfloat16"),
+    "GA": ("sbuf", [128, 512], "bfloat16"),
+    "GB": ("sbuf", [128, 256], "bfloat16"),
+    "GC": ("sbuf", [128, 128], "bfloat16"),
+    "GD": ("sbuf", [128, 128], "bfloat16"),
+    "DA": ("sbuf", [128, 512], "bfloat16"),
+    "DB": ("sbuf", [128, 256], "bfloat16"),
+    "DC": ("sbuf", [128, 128], "bfloat16"),
+    "DD": ("sbuf", [128, 128], "bfloat16"),
+    "X16": ("sbuf", [128, 512], "bfloat16"),
+    "X32": ("sbuf", [128, 256], "bfloat16"),
+    "X64": ("sbuf", [128, 128], "bfloat16"),
     "ZZ": ("sbuf", [128, ZW], "bfloat16"),
+    "ONE": ("sbuf", [128, 128], "bfloat16"),
     "BN": ("sbuf", [128, WB], "bfloat16"),
+    "BN2": ("sbuf", [128, WB], "bfloat16"),
+    "BN4": ("sbuf", [128, 64], "bfloat16"),
     "B15": ("sbuf", [128, WB], "bfloat16"),
     "R": ("sbuf", [128, 128], "bfloat16"),
+    "R2": ("sbuf", [128, 128], "bfloat16"),
+    "R4": ("sbuf", [128, 128], "bfloat16"),
+    "E2": ("sbuf", [128, WB], "bfloat16"),
     "YS": ("sbuf", [128, 128], "bfloat16"),
-    "XP": ("psum", [128, L], "float32"),
+    "XP": ("psum", [128, 512], "float32"),
+    "XPB": ("psum", [128, 512], "float32"),
+    "XC": ("psum", [128, 512], "float32"),
+    "PB2": ("psum", [128, 512], "float32"),
+    "PB4": ("psum", [128, 512], "float32"),
     "ACC": ("psum", [128, 512], "float32"),
 }
-SEMAPHORES = ["own", "sent", "arrA", "arrB", "zero", "fill", "cst", "xp", "glA", "glB", "vA", "v0", "v1", "v2",
+SEMAPHORES = ["own", "sent", "arr0", "arr1", "arr2", "arr3", "zero", "fill", "one", "cst", "x32", "x64", "r2", "e2", "r4",
+              "xp", "xpb", "xc", "pb2", "pb4", "c2", "c4", "gl0", "gl1", "gl2", "gl3", "vA", "vB", "vC", "vD",
               "mm", "yc", "st"]
 
 
@@ -33,11 +49,15 @@ def rank_program(g, core, T, topo):
         return
     S = T.sem
     cores = T.cores
+    mn = AluOpType.min
 
     g.sync.dma_start(T.gath[0], T.x[:]).then_inc(S.own, 16)
     g.sync.dma_start(T.X16[0:CH, :], T.x[:]).then_inc(S.cst, 16)
+    g.scalar.dma_start(T.X32[0:32, :], T.x[:]).then_inc(S.x32, 16)
+    g.scalar.dma_start(T.X64[0:64, :], T.x[:]).then_inc(S.x64, 16)
 
     g.vector.memset(T.ZZ[:, :], 0.0).then_inc(S.zero, 1)
+    g.vector.memset(T.ONE[0:64, :], 1.0).then_inc(S.one, 1)
     g.vector.wait_ge(S.zero, 1)
     for s in range(8):
         a = 8 + 16 * s
@@ -56,52 +76,85 @@ def rank_program(g, core, T, topo):
     for k in range(2, N):
         common &= topo.mask(core, dests[k])
     engines = [e for e in range(16) if (common >> e) & 1]
-    nA = len(engines)
-    nB = N - 1 - nA
+    nE = len(engines)
+    sizes = [nE, nE // 2, nE // 4, nE // 8]
+    first = [1 + sum(sizes[:w]) for w in range(5)]
 
-    def wave(ks, sem):
+    g.wait_ge(S.own, 16)
+    for w in range(4):
+        per = nE // sizes[w]
         trs = []
-        for e, k in zip(engines, ks):
+        for i in range(sizes[w]):
+            k = first[w] + i
+            m = 0
+            for e in engines[per * i:per * i + per]:
+                m |= 1 << e
             rid, pid = topo.addr(dests[k], core)
-            trs.append(RemoteDMATransfer(dst_ids=[DstId(rid=rid, pnc=pid)], dma_engine_mask=1 << e, remote_sem=sem,
+            trs.append(RemoteDMATransfer(dst_ids=[DstId(rid=rid, pnc=pid)], dma_engine_mask=m, remote_sem=S["arr%d" % w],
                                          srcs=[T.gath[0]], dsts=[T.gath[k]], alu_op=0))
         g.remote_dma_fused(trs, local_sem=S.sent)
 
-    g.wait_ge(S.own, 16)
-    wave(range(1, 1 + nA), S.arrA)
-    wave(range(1 + nA, N), S.arrB)
+    g.wait_ge(S.one, 1)
+    eq = AluOpType.is_equal
+    g.affine_select(T.R2[0:32, :], T.ONE[0:32, :], [[0, 4], [1, 32]], eq, 0.0, 0, -1).then_inc(S.r2, 1)
+    g.affine_select(T.E2[0:32, :], T.ONE[0:32, 0:WB], [[-1, WB]], eq, 0.0, 3, 2).then_inc(S.e2, 1)
+    g.affine_select(T.R4[0:64, :], T.ONE[0:64, :], [[0, 2], [1, 64]], eq, 0.0, 0, -1).then_inc(S.r4, 1)
 
     g.tensor.wait_ge(S.cst, 80)
     g.tensor.matmul(T.XP[:, :], T.R[0:CH, :], T.X16[0:CH, :], True, True).then_inc(S.xp, 1)
     acc = T.ACC[0:64, 0:128]
     for b in range(4):
         g.tensor.matmul(acc, T.B15[0:CH, 3 - b:67 - b], T.X16[0:CH, 128 * b:128 * b + 128], b == 0, False)
+    g.tensor.wait_ge(S.r2, 1)
+    g.tensor.wait_ge(S.x32, 16)
+    g.tensor.matmul(T.XPB[:, 0:256], T.R2[0:32, :], T.X32[0:32, :], True, True).then_inc(S.xpb, 1)
+    g.tensor.wait_ge(S.e2, 1)
+    g.tensor.matmul(T.PB2[:, 0:WB], T.R2[0:32, :], T.E2[0:32, :], True, True).then_inc(S.pb2, 1)
+    g.tensor.wait_ge(S.r4, 1)
+    g.tensor.wait_ge(S.x64, 16)
+    g.tensor.matmul(T.XC[:, 0:128], T.R4[0:64, :], T.X64[0:64, :], True, True).then_inc(S.xc, 1)
+    g.tensor.matmul(T.PB4[:, 0:64], T.R4[0:64, :], T.R4[0:64, 0:64], True, True).then_inc(S.pb4, 1)
 
-    pA, pB = CH * nA, CH * nB
-    g.sync.wait_ge(S.arrA, nA)
-    g.sync.dma_start(T.GA[0:pA, :], T.gath[1:1 + nA]).then_inc(S.glA, 16)
-    g.scalar.wait_ge(S.arrB, nB)
-    g.scalar.dma_start(T.GB[0:pB, :], T.gath[1 + nA:N]).then_inc(S.glB, 16)
+    g.sync.wait_ge(S.arr0, nE)
+    g.sync.dma_start(T.GA[:, :], T.gath[first[0]:first[1]]).then_inc(S.gl0, 16)
+    g.scalar.wait_ge(S.arr1, nE)
+    g.scalar.dma_start(T.GB[:, :], T.gath[first[1]:first[2]]).then_inc(S.gl1, 16)
+    g.sync.wait_ge(S.arr2, nE)
+    g.sync.dma_start(T.GC[:, :], T.gath[first[2]:first[3]]).then_inc(S.gl2, 16)
+    g.scalar.wait_ge(S.arr3, nE)
+    g.scalar.dma_start(T.GD[0:64, :], T.gath[first[3]]).then_inc(S.gl3, 16)
 
     g.vector.wait_ge(S.xp, 1)
-    g.vector.wait_ge(S.glA, 16)
-    g.vector.tensor_tensor(T.DA[0:pA, :], T.GA[0:pA, :], T.XP[0:pA, :], AluOpType.min).then_inc(S.vA, 1)
-    g.vector.wait_ge(S.glB, 16)
-    for i, (a, z) in enumerate(BLOCKS_B):
-        g.vector.tensor_tensor(T.DB[0:pB, a:z], T.GB[0:pB, a:z], T.XP[0:pB, a:z], AluOpType.min).then_inc(S["v%d" % i], 1)
+    g.vector.wait_ge(S.gl0, 16)
+    g.vector.tensor_tensor(T.DA[:, :], T.GA[:, :], T.XP[:, :], mn).then_inc(S.vA, 1)
+    g.vector.wait_ge(S.pb2, 1)
+    g.vector.tensor_scalar(T.BN2[:, :], T.PB2[:, 0:WB], -1.0, None, AluOpType.mult).then_inc(S.c2, 1)
+    g.vector.wait_ge(S.pb4, 1)
+    g.vector.tensor_scalar(T.BN4[:, :], T.PB4[:, 0:64], -1.0, None, AluOpType.mult).then_inc(S.c4, 1)
+    g.vector.wait_ge(S.xpb, 1)
+    g.vector.wait_ge(S.gl1, 16)
+    g.vector.tensor_tensor(T.DB[:, :], T.GB[:, :], T.XPB[:, 0:256], mn).then_inc(S.vB, 1)
+    g.vector.wait_ge(S.xc, 1)
+    g.vector.wait_ge(S.gl2, 16)
+    g.vector.tensor_tensor(T.DC[:, :], T.GC[:, :], T.XC[:, 0:128], mn).then_inc(S.vC, 1)
+    g.vector.wait_ge(S.gl3, 16)
+    g.vector.tensor_tensor(T.DD[0:64, :], T.GD[0:64, :], T.XC[0:64, 0:128], mn).then_inc(S.vD, 1)
 
     g.tensor.wait_ge(S.vA, 1)
     for b in range(4):
-        g.tensor.matmul(acc, T.BN[0:pA, 3 - b:67 - b], T.DA[0:pA, 128 * b:128 * b + 128], False, False)
-    for i, (a, z) in enumerate(BLOCKS_B):
-        g.tensor.wait_ge(S["v%d" % i], 1)
-        for b in range(a // 128, z // 128):
-            mm = g.tensor.matmul(acc, T.BN[0:pB, 3 - b:67 - b], T.DB[0:pB, 128 * b:128 * b + 128], False, b == 3)
-    mm.then_inc(S.mm, 1)
+        g.tensor.matmul(acc, T.BN[:, 3 - b:67 - b], T.DA[:, 128 * b:128 * b + 128], False, False)
+    g.tensor.wait_ge(S.c2, 1)
+    g.tensor.wait_ge(S.vB, 1)
+    for b in range(2):
+        g.tensor.matmul(acc, T.BN2[:, 3 - b:67 - b], T.DB[:, 128 * b:128 * b + 128], False, False)
+    g.tensor.wait_ge(S.c4, 1)
+    g.tensor.wait_ge(S.vC, 1)
+    g.tensor.matmul(acc, T.BN4[:, :], T.DC[:, :], False, True).then_inc(S.mm, 1)
 
+    g.vector.wait_ge(S.vD, 1)
     g.vector.wait_ge(S.mm, 1)
-    g.vector.tensor_copy(T.YS[0:64, :], acc).then_inc(S.yc, 1)
+    g.vector.tensor_tensor(T.YS[0:64, :], acc, T.DD[0:64, :], AluOpType.subtract).then_inc(S.yc, 1)
     g.sync.wait_ge(S.yc, 1)
     g.sync.dma_start(T.y[:], T.YS[0:64, :]).then_inc(S.st, 16)
     g.sync.wait_ge(S.st, 16)
-    g.wait_ge(S.sent, N - 1)
+    g.wait_ge(S.sent, 4 * nE)

from concourse.bass import DstId, RemoteDMATransfer
from concourse.mybir import AluOpType

N = 16
CH = 16
L = 512
WB = 68
ZW = CH * WB

SCRATCH = {
    "gath": ("dram", [N, 128, 64], "bfloat16"),
    "GA": ("sbuf", [128, 512], "bfloat16"),
    "GB": ("sbuf", [128, 256], "bfloat16"),
    "GC": ("sbuf", [128, 128], "bfloat16"),
    "GD": ("sbuf", [128, 128], "bfloat16"),
    "DA": ("sbuf", [128, 512], "bfloat16"),
    "DB": ("sbuf", [128, 256], "bfloat16"),
    "DC": ("sbuf", [128, 128], "bfloat16"),
    "DD": ("sbuf", [128, 128], "bfloat16"),
    "X16": ("sbuf", [128, 512], "bfloat16"),
    "X32": ("sbuf", [128, 256], "bfloat16"),
    "X64": ("sbuf", [128, 128], "bfloat16"),
    "ZZ": ("sbuf", [128, ZW], "bfloat16"),
    "ONE": ("sbuf", [128, 128], "bfloat16"),
    "BN": ("sbuf", [128, WB], "bfloat16"),
    "BN2": ("sbuf", [128, WB], "bfloat16"),
    "BN4": ("sbuf", [128, 64], "bfloat16"),
    "B15": ("sbuf", [128, WB], "bfloat16"),
    "R": ("sbuf", [128, 128], "bfloat16"),
    "R2": ("sbuf", [128, 128], "bfloat16"),
    "R4": ("sbuf", [128, 128], "bfloat16"),
    "E2": ("sbuf", [128, WB], "bfloat16"),
    "YS": ("sbuf", [128, 128], "bfloat16"),
    "XP": ("psum", [128, 512], "float32"),
    "XPB": ("psum", [128, 512], "float32"),
    "XC": ("psum", [128, 512], "float32"),
    "PB2": ("psum", [128, 512], "float32"),
    "PB4": ("psum", [128, 512], "float32"),
    "ACC": ("psum", [128, 512], "float32"),
}
SEMAPHORES = ["own", "sent", "arr0", "arr1", "arr2", "arr3", "zero", "fill", "one", "cst", "x32", "x64", "r2", "e2", "r4",
              "xp", "xpb", "xc", "pb2", "pb4", "c2", "c4", "gl0", "gl1", "gl2", "gl3", "vA", "vB", "vC", "vD",
              "mm", "yc", "st"]


def rank_program(g, core, T, topo):
    rank = T.rank_of(core)
    if rank is None:
        return
    S = T.sem
    cores = T.cores
    mn = AluOpType.min

    g.sync.dma_start(T.gath[0], T.x[:]).then_inc(S.own, 16)
    g.sync.dma_start(T.X16[0:CH, :], T.x[:]).then_inc(S.cst, 16)
    g.scalar.dma_start(T.X32[0:32, :], T.x[:]).then_inc(S.x32, 16)
    g.scalar.dma_start(T.X64[0:64, :], T.x[:]).then_inc(S.x64, 16)

    g.vector.memset(T.ZZ[:, :], 0.0).then_inc(S.zero, 1)
    g.vector.memset(T.ONE[0:64, :], 1.0).then_inc(S.one, 1)
    g.vector.wait_ge(S.zero, 1)
    for s in range(8):
        a = 8 + 16 * s
        g.vector.memset(T.ZZ[64:65, a:a + 129 * 7 + 1:129], 1.0).then_inc(S.fill, 1)
    g.vector.memset(T.ZZ[32:33, 3:ZW:WB + 4], 15.0).then_inc(S.fill, 1)
    g.vector.memset(T.ZZ[0:8, 3:ZW:WB + 4], -1.0).then_inc(S.fill, 1)

    g.scalar.wait_ge(S.fill, 10)
    g.scalar.dma_start(T.R[0:8, :], T.ZZ[64:65, 8:1032]).then_inc(S.cst, 16)
    g.scalar.dma_start(T.R[8:16, :], T.ZZ[64:65, 0:1024]).then_inc(S.cst, 16)
    g.scalar.dma_start(T.B15[0:CH, :], T.ZZ[32:33, :]).then_inc(S.cst, 16)
    g.scalar.dma_start(T.BN[:, :], T.ZZ[0:8, :]).then_inc(S.cst, 16)

    dests = [cores[(rank + k) % N] for k in range(N)]
    common = topo.mask(core, dests[1])
    for k in range(2, N):
        common &= topo.mask(core, dests[k])
    engines = [e for e in range(16) if (common >> e) & 1]
    nE = len(engines)
    sizes = [nE, nE // 2, nE // 4, nE // 8]
    first = [1 + sum(sizes[:w]) for w in range(5)]

    g.wait_ge(S.own, 16)
    for w in range(4):
        per = nE // sizes[w]
        trs = []
        for i in range(sizes[w]):
            k = first[w] + i
            m = 0
            for e in engines[per * i:per * i + per]:
                m |= 1 << e
            rid, pid = topo.addr(dests[k], core)
            trs.append(RemoteDMATransfer(dst_ids=[DstId(rid=rid, pnc=pid)], dma_engine_mask=m, remote_sem=S["arr%d" % w],
                                         srcs=[T.gath[0]], dsts=[T.gath[k]], alu_op=0))
        g.remote_dma_fused(trs, local_sem=S.sent)

    g.wait_ge(S.one, 1)
    eq = AluOpType.is_equal
    g.affine_select(T.R2[0:32, :], T.ONE[0:32, :], [[0, 4], [1, 32]], eq, 0.0, 0, -1).then_inc(S.r2, 1)
    g.affine_select(T.E2[0:32, :], T.ONE[0:32, 0:WB], [[-1, WB]], eq, 0.0, 3, 2).then_inc(S.e2, 1)
    g.affine_select(T.R4[0:64, :], T.ONE[0:64, :], [[0, 2], [1, 64]], eq, 0.0, 0, -1).then_inc(S.r4, 1)

    g.tensor.wait_ge(S.cst, 80)
    g.tensor.matmul(T.XP[:, :], T.R[0:CH, :], T.X16[0:CH, :], True, True).then_inc(S.xp, 1)
    acc = T.ACC[0:64, 0:128]
    for b in range(4):
        g.tensor.matmul(acc, T.B15[0:CH, 3 - b:67 - b], T.X16[0:CH, 128 * b:128 * b + 128], b == 0, False)
    g.tensor.wait_ge(S.r2, 1)
    g.tensor.wait_ge(S.x32, 16)
    g.tensor.matmul(T.XPB[:, 0:256], T.R2[0:32, :], T.X32[0:32, :], True, True).then_inc(S.xpb, 1)
    g.tensor.wait_ge(S.e2, 1)
    g.tensor.matmul(T.PB2[:, 0:WB], T.R2[0:32, :], T.E2[0:32, :], True, True).then_inc(S.pb2, 1)
    g.tensor.wait_ge(S.r4, 1)
    g.tensor.wait_ge(S.x64, 16)
    g.tensor.matmul(T.XC[:, 0:128], T.R4[0:64, :], T.X64[0:64, :], True, True).then_inc(S.xc, 1)
    g.tensor.matmul(T.PB4[:, 0:64], T.R4[0:64, :], T.R4[0:64, 0:64], True, True).then_inc(S.pb4, 1)

    g.sync.wait_ge(S.arr0, nE)
    g.sync.dma_start(T.GA[:, :], T.gath[first[0]:first[1]]).then_inc(S.gl0, 16)
    g.scalar.wait_ge(S.arr1, nE)
    g.scalar.dma_start(T.GB[:, :], T.gath[first[1]:first[2]]).then_inc(S.gl1, 16)
    g.sync.wait_ge(S.arr2, nE)
    g.sync.dma_start(T.GC[:, :], T.gath[first[2]:first[3]]).then_inc(S.gl2, 16)
    g.scalar.wait_ge(S.arr3, nE)
    g.scalar.dma_start(T.GD[0:64, :], T.gath[first[3]]).then_inc(S.gl3, 16)

    g.vector.wait_ge(S.xp, 1)
    g.vector.wait_ge(S.gl0, 16)
    g.vector.tensor_tensor(T.DA[:, :], T.GA[:, :], T.XP[:, :], mn).then_inc(S.vA, 1)
    g.vector.wait_ge(S.pb2, 1)
    g.vector.tensor_scalar(T.BN2[:, :], T.PB2[:, 0:WB], -1.0, None, AluOpType.mult).then_inc(S.c2, 1)
    g.vector.wait_ge(S.pb4, 1)
    g.vector.tensor_scalar(T.BN4[:, :], T.PB4[:, 0:64], -1.0, None, AluOpType.mult).then_inc(S.c4, 1)
    g.vector.wait_ge(S.xpb, 1)
    g.vector.wait_ge(S.gl1, 16)
    g.vector.tensor_tensor(T.DB[:, :], T.GB[:, :], T.XPB[:, 0:256], mn).then_inc(S.vB, 1)
    g.vector.wait_ge(S.xc, 1)
    g.vector.wait_ge(S.gl2, 16)
    g.vector.tensor_tensor(T.DC[:, :], T.GC[:, :], T.XC[:, 0:128], mn).then_inc(S.vC, 1)
    g.vector.wait_ge(S.gl3, 16)
    g.vector.tensor_tensor(T.DD[0:64, :], T.GD[0:64, :], T.XC[0:64, 0:128], mn).then_inc(S.vD, 1)

    g.tensor.wait_ge(S.vA, 1)
    for b in range(4):
        g.tensor.matmul(acc, T.BN[:, 3 - b:67 - b], T.DA[:, 128 * b:128 * b + 128], False, False)
    g.tensor.wait_ge(S.c2, 1)
    g.tensor.wait_ge(S.vB, 1)
    for b in range(2):
        g.tensor.matmul(acc, T.BN2[:, 3 - b:67 - b], T.DB[:, 128 * b:128 * b + 128], False, False)
    g.tensor.wait_ge(S.c4, 1)
    g.tensor.wait_ge(S.vC, 1)
    g.tensor.matmul(acc, T.BN4[:, :], T.DC[:, :], False, True).then_inc(S.mm, 1)

    g.vector.wait_ge(S.vD, 1)
    g.vector.wait_ge(S.mm, 1)
    g.vector.tensor_tensor(T.YS[0:64, :], acc, T.DD[0:64, :], AluOpType.subtract).then_inc(S.yc, 1)
    g.sync.wait_ge(S.yc, 1)
    g.sync.dma_start(T.y[:], T.YS[0:64, :]).then_inc(S.st, 16)
    g.sync.wait_ge(S.st, 16)
    g.wait_ge(S.sent, 4 * nE)
